import numpy as np
CORES = [212,213,468,469]
N = 4
def setup_inputs(rng):
    return {"x": rng.standard_normal((N, 128, 128), dtype=np.float32)}
def reference(x):
    s = x.min(axis=0)
    return {"y": np.broadcast_to(s, (N,) + s.shape)}

@@ -1,0 +1,62 @@
+from concourse.bass import DstId, RemoteDMATransfer
+
+SCRATCH = {
+    "own": ("dram", [2, 128, 64], "float32"),
+    "peer": ("dram", [128, 64], "float32"),
+    "land": ("dram", [2, 128, 64], "float32"),
+}
+SEMAPHORES = ["ld_send", "ld_keep", "xch", "part", "res0", "res1", "sent", "stored"]
+
+OFF_CHIP = 0x00FF
+ON_CHIP = 0xFFFF
+MIN = 3
+
+
+def relay_of(half, T):
+    return (T.cores[half] % 128) + (256 if half == 0 else 0)
+
+
+def rank_program(g, core, T, topo):
+    rank = T.rank_of(core)
+    relays = [relay_of(0, T), relay_of(1, T)]
+
+    if rank is None:
+        if core not in relays:
+            return
+        h = relays.index(core)
+        g.wait_ge(T.sem.part, 16)
+        ids = []
+        for d in T.cores:
+            rid, pid = topo.addr(d, core)
+            ids.append(DstId(rid=rid, pnc=pid))
+        g.remote_dma_fused(
+            [RemoteDMATransfer(dst_ids=ids, dma_engine_mask=OFF_CHIP, remote_sem=T.sem["res%d" % h],
+                               srcs=[T.land[0], T.land[1]], dsts=[T.land[h]] * len(ids), alu_op=MIN)],
+            local_sem=T.sem.sent)
+        g.wait_ge(T.sem.sent, 8)
+        return
+
+    side, k = rank // 2, rank % 2
+    peer = T.cores[rank ^ 1]
+    o = 1 - k
+    g.sync.dma_start(T.own[o], T.x[64 * o:64 * o + 64, :]).then_inc(T.sem.ld_send, 16)
+    g.scalar.dma_start(T.own[k], T.x[64 * k:64 * k + 64, :]).then_inc(T.sem.ld_keep, 16)
+
+    g.wait_ge(T.sem.ld_send, 16)
+    rid, pid = topo.addr(peer, core)
+    g.remote_dma(T.peer[:], T.own[o], T.sem.xch, T.sem.sent, pid, rid, ON_CHIP)
+
+    g.wait_ge(T.sem.ld_keep, 16)
+    g.wait_ge(T.sem.xch, 16)
+    rid, pid = topo.addr(relays[k], core)
+    g.remote_dma_fused(
+        [RemoteDMATransfer(dst_ids=[DstId(rid=rid, pnc=pid)], dma_engine_mask=OFF_CHIP, remote_sem=T.sem.part,
+                           srcs=[T.own[k], T.peer[:]], dsts=[T.land[side]], alu_op=MIN)],
+        local_sem=T.sem.sent)
+    g.wait_ge(T.sem.sent, 24)
+
+    g.sync.wait_ge(T.sem.res0, 8)
+    g.sync.dma_start(T.y[0:64, :], T.land[0]).then_inc(T.sem.stored, 16)
+    g.scalar.wait_ge(T.sem.res1, 8)
+    g.scalar.dma_start(T.y[64:128, :], T.land[1]).then_inc(T.sem.stored, 16)
+    g.wait_ge(T.sem.stored, 32)

@@ -1,62 +1,69 @@
 from concourse.bass import DstId, RemoteDMATransfer
 
+PIECES = 8
 SCRATCH = {
-    "own": ("dram", [2, 128, 64], "float32"),
-    "peer": ("dram", [128, 64], "float32"),
-    "land": ("dram", [2, 128, 64], "float32"),
+    "buf": ("dram", [PIECES, 128, 16], "float32"),
+    "pair": ("dram", [2, 128, 16], "float32"),
 }
-SEMAPHORES = ["ld_send", "ld_keep", "xch", "part", "res0", "res1", "sent", "stored"]
+SEMAPHORES = ["loaded", "xch", "part", "res", "sent", "stored"]
 
 OFF_CHIP = 0x00FF
-ON_CHIP = 0xFFFF
 MIN = 3
 
 
-def relay_of(half, T):
-    return (T.cores[half] % 128) + (256 if half == 0 else 0)
+def dst_id(topo, dst, src):
+    rid, pid = topo.addr(dst, src)
+    return DstId(rid=rid, pnc=pid)
 
 
 def rank_program(g, core, T, topo):
     rank = T.rank_of(core)
-    relays = [relay_of(0, T), relay_of(1, T)]
+    j = core % 8
+    chip_base = core - j
+    rank_chips = sorted(set(c - c % 8 for c in T.cores))
+    in_host = rank_chips[0] % 128
+    relay = (256 if j % 2 == 0 else 0) + in_host + j
 
-    if rank is None:
-        if core not in relays:
-            return
-        h = relays.index(core)
+    if core == relay:
         g.wait_ge(T.sem.part, 16)
-        ids = []
-        for d in T.cores:
-            rid, pid = topo.addr(d, core)
-            ids.append(DstId(rid=rid, pnc=pid))
         g.remote_dma_fused(
-            [RemoteDMATransfer(dst_ids=ids, dma_engine_mask=OFF_CHIP, remote_sem=T.sem["res%d" % h],
-                               srcs=[T.land[0], T.land[1]], dsts=[T.land[h]] * len(ids), alu_op=MIN)],
+            [RemoteDMATransfer(dst_ids=[dst_id(topo, d, core) for d in T.cores], dma_engine_mask=OFF_CHIP,
+                               remote_sem=T.sem.res, srcs=[T.pair[0], T.pair[1]],
+                               dsts=[T.buf[j]] * len(T.cores), alu_op=MIN)],
             local_sem=T.sem.sent)
         g.wait_ge(T.sem.sent, 8)
         return
 
-    side, k = rank // 2, rank % 2
-    peer = T.cores[rank ^ 1]
-    o = 1 - k
-    g.sync.dma_start(T.own[o], T.x[64 * o:64 * o + 64, :]).then_inc(T.sem.ld_send, 16)
-    g.scalar.dma_start(T.own[k], T.x[64 * k:64 * k + 64, :]).then_inc(T.sem.ld_keep, 16)
+    if chip_base not in rank_chips:
+        return
+    side = rank_chips.index(chip_base)
 
-    g.wait_ge(T.sem.ld_send, 16)
-    rid, pid = topo.addr(peer, core)
-    g.remote_dma(T.peer[:], T.own[o], T.sem.xch, T.sem.sent, pid, rid, ON_CHIP)
+    sent = 0
+    if rank is None:
+        g.wait_ge(T.sem.xch, 4)
+        srcs = [T.pair[0], T.pair[1]]
+    else:
+        k = rank % 2
+        g.sync.dma_start(T.buf[:], T.x[:]).then_inc(T.sem.loaded, 16)
+        g.wait_ge(T.sem.loaded, 16)
+        others = [p for p in range(PIECES) if p != j]
+        g.remote_dma_fused(
+            [RemoteDMATransfer(dst_ids=[dst_id(topo, chip_base + p, core)], dma_engine_mask=3 << (2 * i),
+                               remote_sem=T.sem.xch, src=T.buf[p], dst=T.pair[k])
+             for i, p in enumerate(others)],
+            local_sem=T.sem.sent)
+        sent += 2 * len(others)
+        g.wait_ge(T.sem.xch, 2)
+        srcs = [T.buf[j], T.pair[1 - k]]
 
-    g.wait_ge(T.sem.ld_keep, 16)
-    g.wait_ge(T.sem.xch, 16)
-    rid, pid = topo.addr(relays[k], core)
     g.remote_dma_fused(
-        [RemoteDMATransfer(dst_ids=[DstId(rid=rid, pnc=pid)], dma_engine_mask=OFF_CHIP, remote_sem=T.sem.part,
-                           srcs=[T.own[k], T.peer[:]], dsts=[T.land[side]], alu_op=MIN)],
+        [RemoteDMATransfer(dst_ids=[dst_id(topo, relay, core)], dma_engine_mask=OFF_CHIP, remote_sem=T.sem.part,
+                           srcs=srcs, dsts=[T.pair[side]], alu_op=MIN)],
         local_sem=T.sem.sent)
-    g.wait_ge(T.sem.sent, 24)
+    sent += 8
+    g.wait_ge(T.sem.sent, sent)
 
-    g.sync.wait_ge(T.sem.res0, 8)
-    g.sync.dma_start(T.y[0:64, :], T.land[0]).then_inc(T.sem.stored, 16)
-    g.scalar.wait_ge(T.sem.res1, 8)
-    g.scalar.dma_start(T.y[64:128, :], T.land[1]).then_inc(T.sem.stored, 16)
-    g.wait_ge(T.sem.stored, 32)
+    if rank is not None:
+        g.sync.wait_ge(T.sem.res, 8 * PIECES)
+        g.sync.dma_start(T.y[:], T.buf[:]).then_inc(T.sem.stored, 16)
+        g.wait_ge(T.sem.stored, 16)

from concourse.bass import DstId, RemoteDMATransfer

PIECES = 8
SCRATCH = {
    "buf": ("dram", [PIECES, 128, 16], "float32"),
    "pair": ("dram", [2, 128, 16], "float32"),
}
SEMAPHORES = ["loaded", "xch", "part", "res", "sent", "stored"]

OFF_CHIP = 0x00FF
MIN = 3


def dst_id(topo, dst, src):
    rid, pid = topo.addr(dst, src)
    return DstId(rid=rid, pnc=pid)


def rank_program(g, core, T, topo):
    rank = T.rank_of(core)
    j = core % 8
    chip_base = core - j
    rank_chips = sorted(set(c - c % 8 for c in T.cores))
    in_host = rank_chips[0] % 128
    relay = (256 if j % 2 == 0 else 0) + in_host + j

    if core == relay:
        g.wait_ge(T.sem.part, 16)
        g.remote_dma_fused(
            [RemoteDMATransfer(dst_ids=[dst_id(topo, d, core) for d in T.cores], dma_engine_mask=OFF_CHIP,
                               remote_sem=T.sem.res, srcs=[T.pair[0], T.pair[1]],
                               dsts=[T.buf[j]] * len(T.cores), alu_op=MIN)],
            local_sem=T.sem.sent)
        g.wait_ge(T.sem.sent, 8)
        return

    if chip_base not in rank_chips:
        return
    side = rank_chips.index(chip_base)

    sent = 0
    if rank is None:
        g.wait_ge(T.sem.xch, 4)
        srcs = [T.pair[0], T.pair[1]]
    else:
        k = rank % 2
        g.sync.dma_start(T.buf[:], T.x[:]).then_inc(T.sem.loaded, 16)
        g.wait_ge(T.sem.loaded, 16)
        others = [p for p in range(PIECES) if p != j]
        g.remote_dma_fused(
            [RemoteDMATransfer(dst_ids=[dst_id(topo, chip_base + p, core)], dma_engine_mask=3 << (2 * i),
                               remote_sem=T.sem.xch, src=T.buf[p], dst=T.pair[k])
             for i, p in enumerate(others)],
            local_sem=T.sem.sent)
        sent += 2 * len(others)
        g.wait_ge(T.sem.xch, 2)
        srcs = [T.buf[j], T.pair[1 - k]]

    g.remote_dma_fused(
        [RemoteDMATransfer(dst_ids=[dst_id(topo, relay, core)], dma_engine_mask=OFF_CHIP, remote_sem=T.sem.part,
                           srcs=srcs, dsts=[T.pair[side]], alu_op=MIN)],
        local_sem=T.sem.sent)
    sent += 8
    g.wait_ge(T.sem.sent, sent)

    if rank is not None:
        g.sync.wait_ge(T.sem.res, 8 * PIECES)
        g.sync.dma_start(T.y[:], T.buf[:]).then_inc(T.sem.stored, 16)
        g.wait_ge(T.sem.stored, 16)
